import numpy as np, ml_dtypes
CORES = [6,15,38,47]
N = 4
import mx_ref
BF = ml_dtypes.bfloat16
def gentries(a):
    return np.ascontiguousarray(a.reshape(8, 16, -1).transpose(0, 2, 1)).reshape(8, -1)
def gtable(e):
    e = np.asarray(e); return np.ascontiguousarray(e.reshape(8, -1, 16).transpose(0, 2, 1)).reshape(128, -1).astype(np.int32)
def gcols(t, e):
    v = np.concatenate([t.reshape(8, 16, -1, 4), np.zeros((8, 16, 1, 4), BF)], axis=2)
    return np.ascontiguousarray(np.stack([v[g][:, e[g]] for g in range(8)])).reshape(128, -1)
def f(rng, *shape):
    return mx_ref.flush((rng.standard_normal(shape, dtype=np.float32) * np.exp2(rng.integers(-2, 3, shape[:-1] + (1,)))).astype(BF))
def wide(rng, *shape, cols=0):
    v = rng.standard_normal(shape, dtype=np.float32) * np.exp2(rng.integers(-12, 13, shape)).astype(np.float32)
    if cols: v *= np.repeat(np.exp2(rng.integers(-cols, cols + 1, shape[:-2] + (1, shape[-1] // 4))) * (rng.random(shape[:-2] + (1, shape[-1] // 4)) > 0.0625), 4, axis=-1).astype(np.float32)
    return mx_ref.flush(v.astype(BF))
T, O, K = 256, 4, 256
def lists(rng, alike=False, groups=False, ends=False, few=False):
    c = []
    for r in range(N):
        e = rng.integers(0, K, (8, O, 2, 128))
        if groups: e = np.stack([e[0]] * 8)
        if ends: e = rng.permuted(np.resize([0, K - 1], (8, O, 2, 128)), axis=3)
        if few:
            for m in range(2): e[:, :, m] = rng.permutation(np.resize(rng.permutation(K)[:8], 8 * O * 128)).reshape(8, O, 128)
        c.append(gtable(e.reshape(8, -1)))
    if alike: c = [c[0]] * N
    return np.stack(c)
def setup_inputs(rng):
    return {"x": f(rng, N, 128, 4 * T), "book": np.stack([f(rng, 128, 8 * K)] * N), "cw": lists(rng)}
def setup_inputs_alike(rng):
    d = setup_inputs(rng); d["cw"] = lists(rng, alike=True); return d
def setup_inputs_groups(rng):
    d = setup_inputs(rng); d["cw"] = lists(rng, groups=True); return d
def setup_inputs_ends(rng):
    d = setup_inputs(rng); d["cw"] = lists(rng, ends=True); return d
def setup_inputs_few(rng):
    d = setup_inputs(rng); d["cw"] = lists(rng, few=True); return d
def setup_inputs_spread(rng):
    d = setup_inputs(rng); d["x"] = wide(rng, N, 128, 4 * T, cols=8); d["book"] = np.stack([wide(rng, 128, 8 * K, cols=4)] * N); return d
def check_inputs(d):
    b = []
    for r in range(N):
        if d["cw"][r].min() < 0 or d["cw"][r].max() >= K: b.append("cw")
        if d["book"][r].tobytes() != d["book"][0].tobytes(): b.append("book")
    return b
def reference(x, book, cw):
    W = []
    for s in range(N):
        e = gentries(cw[s])
        for o in range(O):
            a, b = [gcols(np.ascontiguousarray(book[s][:, 4 * K * m:4 * K * m + 4 * K]), e[:, (2 * o + m) * 128:(2 * o + m) * 128 + 128]).astype(np.float32) for m in range(2)]
            W.append(mx_ref.quantize((a + b).astype(BF)))
    y = np.zeros((N, 128, N * O * T), np.float32)
    for r in range(N):
        X = mx_ref.quantize(np.ascontiguousarray(x[r]))
        for i in range(N * O): y[r][:, T * i:T * i + T] = mx_ref.matmul(W[i], X)
    return {"y": y}

@@ -1,0 +1,213 @@
+from concourse.bass import DstId, RemoteDMATransfer
+from concourse.mybir import dt, AluOpType, ActivationFunctionType
+
+N, TC, O, K = 4, 256, 4, 256
+CW = 128
+C = 2
+UC = 2 * CW
+NT = 4
+
+PARTS = [("own", 0, 0, 1, 1), ("own", 0, 1, 1, 1), ("own", 1, 0, 2, 2), ("diag", 0, 0, 2, 2), ("diag", 1, 0, 2, 2)]
+ORDER = [("own", 0), ("own", 1), ("mate", 0), ("diag", 0), ("plane", 0), ("mate", 1), ("diag", 1), ("plane", 1)]
+SCALAR = [(0, 0), (0, 1), (0, 2), (0, 3), (1, 0), (1, 1), (1, 2), (1, 3), (2, 0), (2, 1), 0, 1, (3, 0), (3, 1), (4, 0), 2, 3, (4, 1),
+          4, 5, 6, 8, 9, 10, 13, 15]
+VECTOR = [(0, 0), (0, 1), (0, 2), (0, 3), (0, "q"), (1, 0), (1, 1), (1, 2), (1, 3), (1, "q"), "x",
+          (2, 0), (2, 1), "l", (2, 2), (2, 3), (2, "q"), (3, 0), (3, 1), (3, 2), (3, 3), (3, "q"),
+          (4, 0), (4, 1), (4, 2), 7, (4, 3), (4, "q"), 11, 12, 14]
+
+SCRATCH = {
+    "cwb": ("sbuf", [128, O, 2, 8], "int32"),
+    "bk0": ("sbuf", [128, NT * K], "bfloat16"),
+    "bk1": ("sbuf", [128, NT * K], "bfloat16"),
+    "xb": ("sbuf", [128, NT * TC], "bfloat16"),
+    "xq": ("sbuf", [128, TC], "float8_e4m3fn_x4"),
+    "xs": ("sbuf", [128, TC], "uint8"),
+    "ys": ("sbuf", [128, N * O * TC], "float32"),
+    "ps": ("psum", [128, 8 * 512], "float32"),
+}
+SEMAPHORES = ["ldc", "ld0", "ld1", "ldx", "lsti", "lstd", "sx", "sent", "st", "ha", "hb", "hc"]
+SEMAPHORES += ["lsta%d" % _t for _t in range(NT)]
+for _s in range(N):
+    SCRATCH["li%d" % _s] = ("sbuf", [128, C, 2, 16], "uint16")
+    SCRATCH["of%d" % _s] = ("sbuf", [128, C, 4, 32], "uint16")
+    SEMAPHORES += ["l%d" % _s]
+    for _c in range(C):
+        SCRATCH["a%d%d" % (_s, _c)] = ("sbuf", [128, NT * UC], "bfloat16")
+        SCRATCH["w%d%d" % (_s, _c)] = ("sbuf", [128, NT * UC], "bfloat16")
+        SCRATCH["q%d%d" % (_s, _c)] = ("sbuf", [128, UC], "float8_e4m3fn_x4")
+        SCRATCH["s%d%d" % (_s, _c)] = ("sbuf", [128, UC], "uint8")
+        SEMAPHORES += ["r%d%d" % (_s, _c)]
+for _p in range(len(PARTS)):
+    SEMAPHORES += ["pa%d%d" % (_p, _t) for _t in range(NT)] + ["pv%d" % _p, "pq%d" % _p]
+for _k in range(N * O):
+    SEMAPHORES += ["m%d" % _k, "e%d" % _k]
+
+
+def relation(topo, a, b):
+    ca, cb = topo.chip(a), topo.chip(b)
+    return "mate" if topo.mates(ca, cb) else "plane" if topo.same_plane(ca, cb) else "diag"
+
+
+def helper(topo, core, far):
+    return [c for c in topo.cores_of(core) if topo.die(c) != topo.die(core) and topo.may_write(c, far)][0]
+
+
+def rank_program(g, core, T, topo):
+    S = T.sem
+    me = T.rank_of(core)
+    owner = me
+    if me is None:
+        for r in range(N):
+            if core in topo.cores_of(T.cores[r]):
+                owner = r
+        if owner is None:
+            return
+    home = T.cores[owner]
+    by = {relation(topo, home, T.cores[r]): r for r in range(N) if r != owner}
+    at = {k: T.cores[by[k]] for k in by}
+    hlp = helper(topo, home, at["plane"])
+
+    def transfer(src, cores, sem, es):
+        ids = [DstId(rid=topo.addr(c)[0], pnc=topo.addr(c)[1]) for c in cores]
+        return RemoteDMATransfer(dst_ids=ids, dma_engine_mask=sum(1 << e for e in es), remote_sem=S[sem], srcs=[src],
+                                 dsts=[src] * len(ids))
+
+    Q0, S0 = T["q%d0" % owner], T["s%d0" % owner]
+    early = [("ha", Q0[:, 0:CW].bitcast(dt.uint8)), ("hb", Q0[:, CW:UC].bitcast(dt.uint8)), ("hc", S0[:, :])]
+    far = topo.engines(home, at["mate"])
+    near = [e for e in topo.engines(home, hlp) if e not in far]
+
+    if me is None:
+        if core == hlp:
+            es = topo.engines(core, at["plane"])
+            for sem, src in early:
+                g.wait_ge(S[sem], len(near))
+                g.remote_dma_fused([transfer(src, [at["plane"]], "r%d0" % owner, es)], local_sem=S.sent)
+            g.wait_ge(S.sent, len(early) * len(es))
+        return
+    v, a, te, sy = g.vector, g.scalar, g.tensor, g.sync
+    who = dict(by)
+    who["own"] = me
+    nfar = {w: len(topo.engines(T.cores[by[w]], core)) for w in by}
+
+    sy.dma_start(T.cwb[:], T.cw[:, :]).then_inc(S.ldc, 16)
+    sy.dma_start(T.bk0[:, :], T.book[:, 0:NT * K]).then_inc(S.ld0, 16)
+    sy.dma_start(T.bk1[:, :], T.book[:, NT * K:2 * NT * K]).then_inc(S.ld1, 16)
+    sy.dma_start(T.xb[:, :], T.x[:, :]).then_inc(S.ldx, 16)
+
+    def tables(s, sems):
+        for t in range(NT):
+            v.tensor_scalar(T["of%d" % s][:, :, t // 2:4:2, 16 * (t % 2):16 * (t % 2) + 16], T["li%d" % s][:, :, :, :], t, None,
+                            AluOpType.add).then_inc(S[sems[t]], 1)
+
+    v.wait_ge(S.ldc, 16)
+    li = T["li%d" % me]
+    for m in range(2):
+        v.tensor_scalar(li[:, :, m, :], T.cwb[:, :, m, :], NT, None, AluOpType.mult).then_inc(S.lsti, 1)
+    v.wait_ge(S.lsti, 2)
+    tables(me, ["lsta%d" % t for t in range(NT)])
+
+    nsent = 0
+    g.wait_ge(S.lsti, 2)
+    es = topo.engines(core, at["diag"])
+    g.remote_dma_fused([transfer(li[:, :, :, :], [at["diag"]], "l%d" % me, es)], local_sem=S.sent)
+    nsent += len(es)
+    for i, (sem, src) in enumerate(early):
+        if i < 2:
+            g.wait_ge(S["pq%d" % i], 1)
+        g.remote_dma_fused([transfer(src, [at["mate"]], "r%d0" % me, far), transfer(src, [hlp], sem, near)], local_sem=S.sent)
+        nsent += len(far) + len(near)
+    g.wait_ge(S.pq2, 1)
+    for src in (T["q%d1" % me][:, :].bitcast(dt.uint8), T["s%d1" % me][:, :]):
+        g.remote_dma_fused([transfer(src, [at["plane"], at["mate"]], "r%d1" % me, far)], local_sem=S.sent)
+        nsent += len(far)
+    g.wait_ge(S.sent, nsent)
+
+    def col(k):
+        w, c = ORDER[k // 2]
+        return (who[w] * O + 2 * c + k % 2) * TC
+
+    def take(k):
+        return T.ys[:, col(k):col(k) + TC], T.ps[:, k % 8 * 512:k % 8 * 512 + TC]
+
+    seen = {}
+
+    def once(q, key, sem, n):
+        if (key, sem) not in seen:
+            seen[(key, sem)] = 1
+            q.wait_ge(S[sem], n)
+
+    a.wait_ge(S.ld0, 16)
+    for it in SCALAR:
+        if isinstance(it, int):
+            a.wait_ge(S["m%d" % it], 1)
+            dst, src = take(it)
+            a.activation(dst, src, ActivationFunctionType.Copy).then_inc(S["e%d" % it], 1)
+            continue
+        p, i = it
+        w, c, h, nh, nt = PARTS[p]
+        s = who[w]
+        for t in range(i * nt, (i + 1) * nt):
+            if w == "own":
+                once(a, "a", "lsta%d" % t, 1)
+            else:
+                once(a, "a", "lstd", NT)
+        A, of = T["a%d%d" % (s, c)], T["of%d" % s]
+        t = i * nt
+        off = of[:, c, t // 2, :] if nt == 2 else of[:, c, t // 2, 16 * (t % 2) + 8 * h:16 * (t % 2) + 8 * (h + nh)]
+        a.activation(A[:, t * UC + h * CW:(t + nt - 1) * UC + (h + nh) * CW], T.bk0[:, :].indirect(off),
+                     ActivationFunctionType.Copy).then_inc(S["pa%d%d" % (p, i)], 1)
+
+    for t in range(NT):
+        v.wait_ge(S["lsta%d" % t], 1)
+    v.wait_ge(S.ld1, 16)
+    for it in VECTOR:
+        if it == "x":
+            v.wait_ge(S.ldx, 16)
+            v.quantize_mx(T.xq[:, :], T.xs[:, :], T.xb[:, :]).then_inc(S.sx, 1)
+            continue
+        if it == "l":
+            v.wait_ge(S["l%d" % by["diag"]], nfar["diag"])
+            tables(by["diag"], ["lstd"] * NT)
+            continue
+        if isinstance(it, int):
+            v.wait_ge(S["m%d" % it], 1)
+            dst, src = take(it)
+            v.tensor_copy(dst, src).then_inc(S["e%d" % it], 1)
+            continue
+        p, t = it
+        w, c, h, nh, nt = PARTS[p]
+        s = who[w]
+        A, W, of = T["a%d%d" % (s, c)], T["w%d%d" % (s, c)], T["of%d" % s]
+        lo, hi = h * CW, (h + nh) * CW
+        if t == "q":
+            v.wait_ge(S["pv%d" % p], NT)
+            v.quantize_mx(T["q%d%d" % (s, c)][:, lo:hi], T["s%d%d" % (s, c)][:, lo:hi], W[:, NT * lo:NT * hi]).then_inc(S["pq%d" % p], 1)
+            continue
+        if w != "own":
+            once(v, "v", "lstd", NT)
+        once(v, "v", "pa%d%d" % (p, t // nt), 1)
+        off = of[:, c, 2 + t // 2, 16 * (t % 2) + 8 * h:16 * (t % 2) + 8 * (h + nh)]
+        v.tensor_tensor(W[:, NT * lo + t:NT * hi:NT], T.bk1[:, :].indirect(off), A[:, t * UC + lo:t * UC + hi],
+                        AluOpType.add).then_inc(S["pv%d" % p], 1)
+
+    te.wait_ge(S.sx, 1)
+    for k in range(N * O):
+        w, c = ORDER[k // 2]
+        h = k % 2
+        s = who[w]
+        if w in ("own", "diag"):
+            for p, (w2, c2, h2, nh, nt) in enumerate(PARTS):
+                if (w2, c2) == (w, c) and h2 <= h < h2 + nh:
+                    once(te, "t", "pq%d" % p, 1)
+        else:
+            once(te, "t", "r%d%d" % (s, c), (len(early) if c == 0 else 2) * nfar[w])
+        if k >= 8:
+            te.wait_ge(S["e%d" % (k - 8)], 1)
+        te.matmul_mx(T.ps[:, k % 8 * 512:k % 8 * 512 + TC], T["q%d%d" % (s, c)][:, h * CW:(h + 1) * CW],
+                     T["s%d%d" % (s, c)][:, h * CW:(h + 1) * CW], T.xq[:, :], T.xs[:, :], True, True).then_inc(S["m%d" % k], 1)
+    for k in range(0, N * O, 2):
+        sy.wait_ge(S["e%d" % k], 1)
+        sy.wait_ge(S["e%d" % (k + 1)], 1)
+        sy.dma_start(T.y[:, col(k):col(k) + 2 * TC], T.ys[:, col(k):col(k) + 2 * TC]).then_inc(S.st, 16)
+    sy.wait_ge(S.st, 16 * (N * O // 2))

@@ -3,20 +3,29 @@ from concourse.mybir import dt, AluOpType, ActivationFunctionType
 
 N, TC, O, K = 4, 256, 4, 256
 CW = 128
-C = 2
-UC = 2 * CW
 NT = 4
+LC = CW // 16
 
-PARTS = [("own", 0, 0, 1, 1), ("own", 0, 1, 1, 1), ("own", 1, 0, 2, 2), ("diag", 0, 0, 2, 2), ("diag", 1, 0, 2, 2)]
-ORDER = [("own", 0), ("own", 1), ("mate", 0), ("diag", 0), ("plane", 0), ("mate", 1), ("diag", 1), ("plane", 1)]
-SCALAR = [(0, 0), (0, 1), (0, 2), (0, 3), (1, 0), (1, 1), (1, 2), (1, 3), (2, 0), (2, 1), 0, 1, (3, 0), (3, 1), (4, 0), 2, 3, (4, 1),
-          4, 5, 6, 8, 9, 10, 13, 15]
-VECTOR = [(0, 0), (0, 1), (0, 2), (0, 3), (0, "q"), (1, 0), (1, 1), (1, 2), (1, 3), (1, "q"), "x",
-          (2, 0), (2, 1), "l", (2, 2), (2, 3), (2, "q"), (3, 0), (3, 1), (3, 2), (3, 3), (3, "q"),
-          (4, 0), (4, 1), (4, 2), 7, (4, 3), (4, "q"), 11, 12, 14]
+HOLD = (None, None)
+PARTS = [("own", 0, 1, 1), ("own", 1, 1, 2), ("own", 2, 2, 2), ("plane", 2, 1, 4), ("plane", 3, 1, 4), ("diag", 3, 1, 4)]
+LISTS = (1, 2, 2)
+WAYS = {0: {"own": [("far", ["plane"]), ("near0", ["own.o0"]), ("near1", ["own.s0"])],
+            "own.o0": [("far", ["diag"])], "own.s0": [("far", ["mate"])]},
+        1: {"own": [("far", ["mate"])]},
+        2: {"own": [("far", ["plane"]), ("near0", ["own.o0"]), ("near1", ["own.o1"])],
+            "own.o0": [("far", ["diag"])], "own.o1": [("far", ["mate"])]}}
+PIECES = [("q", "own", 0, 1, 2), ("q", "own", 1, 1, 0), ("s", "own", 0, 2, 0),
+          ("q", "own", 2, 2, 1), ("s", "own", 2, 2, 1), ("q", "plane", 2, 1, 1), ("s", "plane", 2, 1, 1)]
+GPSIMD = [("own", _i) for _i in range(len(PIECES))]
+ORDER = [("own", 0), ("own", 1), ("own", 2), ("own", 3), ("plane", 0), ("plane", 1), ("plane", 2), ("plane", 3),
+         ("mate", 2), ("mate", 3), ("mate", 0), ("mate", 1), ("diag", 0), ("diag", 1), ("diag", 2), ("diag", 3)]
+SCALAR = [(0, 0), (0, 2), (0, 3), (1, 0), (1, 1), (2, 0), (2, 1), 0, 1, (3, 0), (4, 0), 2, (5, 0),
+          3, 4, 5, 6, 7, 8, 9, 11, 13, 15]
+VECTOR = [(0, 1), "p0", "p1", "x", "p2", "p3", "p4", "p5", 10, 12, 14]
+STORE = 16
 
 SCRATCH = {
-    "cwb": ("sbuf", [128, O, 2, 8], "int32"),
+    "cwb": ("sbuf", [128, O, 2, LC], "int32"),
     "bk0": ("sbuf", [128, NT * K], "bfloat16"),
     "bk1": ("sbuf", [128, NT * K], "bfloat16"),
     "xb": ("sbuf", [128, NT * TC], "bfloat16"),
@@ -24,111 +33,73 @@ SCRATCH = {
     "xs": ("sbuf", [128, TC], "uint8"),
     "ys": ("sbuf", [128, N * O * TC], "float32"),
     "ps": ("psum", [128, 8 * 512], "float32"),
+    "of1": ("sbuf", [128, O, 2, NT * LC], "uint16"),
+    "li": ("sbuf", [128, O // 2, 2, 2 * LC], "uint16"),
+    "of2": ("sbuf", [128, O // 2, 2, NT * 2 * LC], "uint16"),
 }
-SEMAPHORES = ["ldc", "ld0", "ld1", "ldx", "lsti", "lstd", "sx", "sent", "st", "ha", "hb", "hc"]
-SEMAPHORES += ["lsta%d" % _t for _t in range(NT)]
+SEMAPHORES = ["ldc", "ld0", "ld1", "ldx", "lst", "lst1", "lst2", "lstr", "sx", "sent", "st", "hold"]
 for _s in range(N):
-    SCRATCH["li%d" % _s] = ("sbuf", [128, C, 2, 16], "uint16")
-    SCRATCH["of%d" % _s] = ("sbuf", [128, C, 4, 32], "uint16")
-    SEMAPHORES += ["l%d" % _s]
-    for _c in range(C):
-        SCRATCH["a%d%d" % (_s, _c)] = ("sbuf", [128, NT * UC], "bfloat16")
-        SCRATCH["w%d%d" % (_s, _c)] = ("sbuf", [128, NT * UC], "bfloat16")
-        SCRATCH["q%d%d" % (_s, _c)] = ("sbuf", [128, UC], "float8_e4m3fn_x4")
-        SCRATCH["s%d%d" % (_s, _c)] = ("sbuf", [128, UC], "uint8")
-        SEMAPHORES += ["r%d%d" % (_s, _c)]
+    SCRATCH["q%d" % _s] = ("sbuf", [128, O * CW], "float8_e4m3fn_x4")
+    SCRATCH["s%d" % _s] = ("sbuf", [128, O * CW], "uint8")
+    SEMAPHORES += ["r%s%d%d" % (_k, _s, _o) for _o in range(O) for _k in "qs"]
 for _p in range(len(PARTS)):
+    SCRATCH["a%d" % _p] = ("sbuf", [128, NT * CW * PARTS[_p][2]], "bfloat16")
+    SCRATCH["w%d" % _p] = ("sbuf", [128, NT * CW * PARTS[_p][2]], "bfloat16")
     SEMAPHORES += ["pa%d%d" % (_p, _t) for _t in range(NT)] + ["pv%d" % _p, "pq%d" % _p]
+FOREIGN = sorted(set(_p[0] for _p in PARTS) - {"own"})
+for _w in FOREIGN:
+    SCRATCH["of" + _w] = ("sbuf", [128, LISTS[2], 2, NT * LC] if LISTS[0] == 1 else [128, LISTS[2] // 2, 2, NT * 2 * LC],
+                          "uint16")
+    SEMAPHORES += ["l" + _w]
 for _k in range(N * O):
     SEMAPHORES += ["m%d" % _k, "e%d" % _k]
+RELS = ["own", "mate", "plane", "diag"]
 
 
 def relation(topo, a, b):
     ca, cb = topo.chip(a), topo.chip(b)
-    return "mate" if topo.mates(ca, cb) else "plane" if topo.same_plane(ca, cb) else "diag"
-
-
-def helper(topo, core, far):
-    return [c for c in topo.cores_of(core) if topo.die(c) != topo.die(core) and topo.may_write(c, far)][0]
+    return "own" if a == b else "mate" if topo.mates(ca, cb) else "plane" if topo.same_plane(ca, cb) else "diag"
 
 
 def rank_program(g, core, T, topo):
     S = T.sem
-    me = T.rank_of(core)
-    owner = me
-    if me is None:
-        for r in range(N):
-            if core in topo.cores_of(T.cores[r]):
-                owner = r
-        if owner is None:
-            return
-    home = T.cores[owner]
-    by = {relation(topo, home, T.cores[r]): r for r in range(N) if r != owner}
-    at = {k: T.cores[by[k]] for k in by}
-    hlp = helper(topo, home, at["plane"])
+    who = [{relation(topo, T.cores[r], T.cores[s]): s for s in range(N)} for r in range(N)]
+    named = []
+    for r in range(N):
+        names = {}
+        for w in RELS:
+            home = names[w] = T.cores[who[r][w]]
+            mate = T.cores[who[who[r][w]]["mate"]]
+            for key, same in (("o", False), ("s", True)):
+                cs = [c for c in topo.cores_of(home) if c != home and (topo.die(c) == topo.die(home)) == same]
+                cs.sort(key=lambda c: not topo.may_write(c, mate))
+                for i, c in enumerate(cs):
+                    names["%s.%s%d" % (w, key, i)] = c
+        named.append(names)
+    far = topo.engines(named[0]["own"], named[0]["mate"])
+    near = [e for e in topo.engines(named[0]["own"], named[0]["own.o0"]) if e not in far]
+    sets = {"far": far, "near": near, "all": far + near}
+    for key in ("far", "near"):
+        h = len(sets[key]) // 2
+        sets[key + "0"], sets[key + "1"] = sets[key][:h], sets[key][h:]
 
-    def transfer(src, cores, sem, es):
+    def transfer(src, dst, cores, sem, es):
         ids = [DstId(rid=topo.addr(c)[0], pnc=topo.addr(c)[1]) for c in cores]
         return RemoteDMATransfer(dst_ids=ids, dma_engine_mask=sum(1 << e for e in es), remote_sem=S[sem], srcs=[src],
-                                 dsts=[src] * len(ids))
+                                 dsts=[dst] * len(ids))
 
-    Q0, S0 = T["q%d0" % owner], T["s%d0" % owner]
-    early = [("ha", Q0[:, 0:CW].bitcast(dt.uint8)), ("hb", Q0[:, CW:UC].bitcast(dt.uint8)), ("hc", S0[:, :])]
-    far = topo.engines(home, at["mate"])
-    near = [e for e in topo.engines(home, hlp) if e not in far]
+    comes = {}
+    for r in range(N):
+        for kind, w, o, n, way in PIECES:
+            for snd in WAYS[way]:
+                for es, to in WAYS[way][snd]:
+                    if core in [named[r][d] for d in to]:
+                        for j in range(o, o + n):
+                            comes[(kind, who[r][w], j)] = ("r%s%d%d" % (kind, who[r][w], o), len(sets[es]))
+    nsent = [0]
 
-    if me is None:
-        if core == hlp:
-            es = topo.engines(core, at["plane"])
-            for sem, src in early:
-                g.wait_ge(S[sem], len(near))
-                g.remote_dma_fused([transfer(src, [at["plane"]], "r%d0" % owner, es)], local_sem=S.sent)
-            g.wait_ge(S.sent, len(early) * len(es))
-        return
-    v, a, te, sy = g.vector, g.scalar, g.tensor, g.sync
-    who = dict(by)
-    who["own"] = me
-    nfar = {w: len(topo.engines(T.cores[by[w]], core)) for w in by}
-
-    sy.dma_start(T.cwb[:], T.cw[:, :]).then_inc(S.ldc, 16)
-    sy.dma_start(T.bk0[:, :], T.book[:, 0:NT * K]).then_inc(S.ld0, 16)
-    sy.dma_start(T.bk1[:, :], T.book[:, NT * K:2 * NT * K]).then_inc(S.ld1, 16)
-    sy.dma_start(T.xb[:, :], T.x[:, :]).then_inc(S.ldx, 16)
-
-    def tables(s, sems):
-        for t in range(NT):
-            v.tensor_scalar(T["of%d" % s][:, :, t // 2:4:2, 16 * (t % 2):16 * (t % 2) + 16], T["li%d" % s][:, :, :, :], t, None,
-                            AluOpType.add).then_inc(S[sems[t]], 1)
-
-    v.wait_ge(S.ldc, 16)
-    li = T["li%d" % me]
-    for m in range(2):
-        v.tensor_scalar(li[:, :, m, :], T.cwb[:, :, m, :], NT, None, AluOpType.mult).then_inc(S.lsti, 1)
-    v.wait_ge(S.lsti, 2)
-    tables(me, ["lsta%d" % t for t in range(NT)])
-
-    nsent = 0
-    g.wait_ge(S.lsti, 2)
-    es = topo.engines(core, at["diag"])
-    g.remote_dma_fused([transfer(li[:, :, :, :], [at["diag"]], "l%d" % me, es)], local_sem=S.sent)
-    nsent += len(es)
-    for i, (sem, src) in enumerate(early):
-        if i < 2:
-            g.wait_ge(S["pq%d" % i], 1)
-        g.remote_dma_fused([transfer(src, [at["mate"]], "r%d0" % me, far), transfer(src, [hlp], sem, near)], local_sem=S.sent)
-        nsent += len(far) + len(near)
-    g.wait_ge(S.pq2, 1)
-    for src in (T["q%d1" % me][:, :].bitcast(dt.uint8), T["s%d1" % me][:, :]):
-        g.remote_dma_fused([transfer(src, [at["plane"], at["mate"]], "r%d1" % me, far)], local_sem=S.sent)
-        nsent += len(far)
-    g.wait_ge(S.sent, nsent)
-
-    def col(k):
-        w, c = ORDER[k // 2]
-        return (who[w] * O + 2 * c + k % 2) * TC
-
-    def take(k):
-        return T.ys[:, col(k):col(k) + TC], T.ps[:, k % 8 * 512:k % 8 * 512 + TC]
+    def part(w, o):
+        return [p for p, (w2, o2, n, nt) in enumerate(PARTS) if w2 == w and o2 <= o < o2 + n]
 
     seen = {}
 
@@ -137,77 +108,167 @@ def rank_program(g, core, T, topo):
             seen[(key, sem)] = 1
             q.wait_ge(S[sem], n)
 
-    a.wait_ge(S.ld0, 16)
+    def send(r, i, snd):
+        kind, w, o, n, way = PIECES[i]
+        s = who[r][w]
+        src = T["%s%d" % (kind, s)][:, o * CW:(o + n) * CW]
+        if kind == "q":
+            src = src.bitcast(dt.uint8)
+        for j in range(o, o + n):
+            if snd != "own":
+                once(g, "g", *comes[(kind, s, j)])
+            else:
+                once(g, "g", "pq%d" % part(w, j)[0], 1)
+        g.remote_dma_fused([transfer(src, src, [named[r][d] for d in to], "r%s%d%d" % (kind, s, o), sets[es])
+                            for es, to in WAYS[way][snd]], local_sem=S.sent)
+        nsent[0] += sum(len(sets[es]) for es, to in WAYS[way][snd])
+
+    me = T.rank_of(core)
+    if me is None:
+        for i in range(len(PIECES)):
+            for snd in WAYS[PIECES[i][4]]:
+                for r in range(N):
+                    if named[r][snd] == core:
+                        send(r, i, snd)
+        if nsent[0]:
+            g.wait_ge(S.sent, nsent[0])
+        return
+    v, a, te, sy = g.vector, g.scalar, g.tensor, g.sync
+    by = who[me]
+    nl = len(far) // max(1, len(FOREIGN))
+
+    sy.dma_start(T.cwb[:], T.cw[:, :]).then_inc(S.ldc, 16)
+    sy.dma_start(T.bk0[:, :], T.book[:, 0:NT * K]).then_inc(S.ld0, 16)
+    sy.dma_start(T.bk1[:, :], T.book[:, NT * K:2 * NT * K]).then_inc(S.ld1, 16)
+    sy.dma_start(T.xb[:, :], T.x[:, :]).then_inc(S.ldx, 16)
+
+    if LISTS:
+        lw, lo, ln = LISTS
+        g.wait_ge(S.lst1 if lw == 1 else S.lst2, NT)
+        src = T.of1[:, lo:lo + ln, :, :] if lw == 1 else T.of2[:, lo // 2:(lo + ln) // 2, :, :]
+        g.remote_dma_fused([transfer(src, T["of" + w][:], [named[me][w]], "l" + w,
+                                     far[i * nl:(i + 1) * nl]) for i, w in enumerate(FOREIGN)], local_sem=S.sent)
+        nsent[0] += len(far)
+    for snd, p in GPSIMD:
+        send(by[snd], p, snd)
+        if p == HOLD[1]:
+            g.sem_inc(S.hold, 1)
+    g.wait_ge(S.sent, nsent[0])
+
+    def col(k):
+        w, o = ORDER[k]
+        return (by[w] * O + o) * TC
+
+    def take(k):
+        return T.ys[:, col(k):col(k) + TC], T.ps[:, k % 8 * 512:k % 8 * 512 + TC]
+
+    def offsets(q, key, p, m, t, nt):
+        w, o, n, _ = PARTS[p]
+        if w == "own" and n == 1 and (nt > 1 or LISTS[0] == 1):
+            once(q, key, "lst1", NT)
+            return T.of1[:, o, m, t * LC:(t + nt) * LC]
+        if w != "own" and LISTS[0] == 1:
+            once(q, key, "l" + w, nl)
+            return T["of" + w][:, o - LISTS[1], m, t * LC:(t + nt) * LC]
+        if w == "own":
+            once(q, key, "lst2", NT)
+            of = T.of2
+        else:
+            once(q, key, "l" + w, nl)
+            of, o = T["of" + w], o - LISTS[1]
+        c0 = (2 * t + o % 2) * LC
+        return of[:, o // 2, m, c0:c0 + n * nt * LC]
+
+    def gather0(q, key, p, i):
+        w, o, n, nt = PARTS[p]
+        once(q, key, "ld0", 16)
+        off = offsets(q, key, p, 0, i * nt, nt)
+        return T["a%d" % p][:, i * nt * n * CW:(i + 1) * nt * n * CW], T.bk0[:, :].indirect(off)
+
     for it in SCALAR:
         if isinstance(it, int):
             a.wait_ge(S["m%d" % it], 1)
             dst, src = take(it)
             a.activation(dst, src, ActivationFunctionType.Copy).then_inc(S["e%d" % it], 1)
-            continue
-        p, i = it
-        w, c, h, nh, nt = PARTS[p]
-        s = who[w]
-        for t in range(i * nt, (i + 1) * nt):
-            if w == "own":
-                once(a, "a", "lsta%d" % t, 1)
-            else:
-                once(a, "a", "lstd", NT)
-        A, of = T["a%d%d" % (s, c)], T["of%d" % s]
-        t = i * nt
-        off = of[:, c, t // 2, :] if nt == 2 else of[:, c, t // 2, 16 * (t % 2) + 8 * h:16 * (t % 2) + 8 * (h + nh)]
-        a.activation(A[:, t * UC + h * CW:(t + nt - 1) * UC + (h + nh) * CW], T.bk0[:, :].indirect(off),
-                     ActivationFunctionType.Copy).then_inc(S["pa%d%d" % (p, i)], 1)
+        else:
+            dst, src = gather0(a, "a", *it)
+            a.activation(dst, src, ActivationFunctionType.Copy).then_inc(S["pa%d%d" % it], 1)
 
-    for t in range(NT):
-        v.wait_ge(S["lsta%d" % t], 1)
-    v.wait_ge(S.ld1, 16)
+    v.wait_ge(S.ldc, 16)
+
+    def tables1():
+        for t in range(NT):
+            v.tensor_scalar(T.of1[:, :, :, t * LC:(t + 1) * LC], T.cwb[:, :, :, :], NT, t, AluOpType.mult,
+                            AluOpType.add).then_inc(S.lst1, 1)
+
+    def tables2():
+        for m in range(2):
+            v.tensor_scalar(T.li[:, :, m, :], T.cwb[:, :, m, :], NT, None, AluOpType.mult).then_inc(S.lst, 1)
+        v.wait_ge(S.lst, 2)
+        for t in range(NT):
+            v.tensor_scalar(T.of2[:, :, :, 2 * t * LC:2 * (t + 1) * LC], T.li[:, :, :, :], t, None, AluOpType.add).then_inc(S.lst2, 1)
+
+    if LISTS[0] == 1:
+        tables1()
+        if [p for p in PARTS if p[2] == 2]:
+            tables2()
+    else:
+        tables2()
+        if [p for p in PARTS if p[2] == 1 and p[3] > 1]:
+            tables1()
     for it in VECTOR:
         if it == "x":
             v.wait_ge(S.ldx, 16)
             v.quantize_mx(T.xq[:, :], T.xs[:, :], T.xb[:, :]).then_inc(S.sx, 1)
-            continue
-        if it == "l":
-            v.wait_ge(S["l%d" % by["diag"]], nfar["diag"])
-            tables(by["diag"], ["lstd"] * NT)
-            continue
-        if isinstance(it, int):
+        elif isinstance(it, int):
             v.wait_ge(S["m%d" % it], 1)
             dst, src = take(it)
             v.tensor_copy(dst, src).then_inc(S["e%d" % it], 1)
-            continue
-        p, t = it
-        w, c, h, nh, nt = PARTS[p]
-        s = who[w]
-        A, W, of = T["a%d%d" % (s, c)], T["w%d%d" % (s, c)], T["of%d" % s]
-        lo, hi = h * CW, (h + nh) * CW
-        if t == "q":
+        elif isinstance(it, tuple):
+            dst, src = gather0(v, "v", *it)
+            v.tensor_copy(dst, src).then_inc(S["pa%d%d" % it], 1)
+        else:
+            p = int(it[1])
+            w, o, n, nt = PARTS[p]
+            A, W = T["a%d" % p], T["w%d" % p]
+            once(v, "v", "ld1", 16)
+            for t in {"p": range(NT), "q": [], "g": [int(it[-1])]}[it[0]]:
+                off = offsets(v, "v", p, 1, t, 1)
+                once(v, "v", "pa%d%d" % (p, t // nt), 1)
+                v.tensor_tensor(W[:, t::NT], T.bk1[:, :].indirect(off), A[:, t * n * CW:(t + 1) * n * CW],
+                                AluOpType.add).then_inc(S["pv%d" % p], 1)
+            if it[0] == "g":
+                continue
             v.wait_ge(S["pv%d" % p], NT)
-            v.quantize_mx(T["q%d%d" % (s, c)][:, lo:hi], T["s%d%d" % (s, c)][:, lo:hi], W[:, NT * lo:NT * hi]).then_inc(S["pq%d" % p], 1)
-            continue
-        if w != "own":
-            once(v, "v", "lstd", NT)
-        once(v, "v", "pa%d%d" % (p, t // nt), 1)
-        off = of[:, c, 2 + t // 2, 16 * (t % 2) + 8 * h:16 * (t % 2) + 8 * (h + nh)]
-        v.tensor_tensor(W[:, NT * lo + t:NT * hi:NT], T.bk1[:, :].indirect(off), A[:, t * UC + lo:t * UC + hi],
-                        AluOpType.add).then_inc(S["pv%d" % p], 1)
+            s = by[w]
+            v.quantize_mx(T["q%d" % s][:, o * CW:(o + n) * CW], T["s%d" % s][:, o * CW:(o + n) * CW],
+                          W[:, :]).then_inc(S["pq%d" % p], 1)
 
     te.wait_ge(S.sx, 1)
     for k in range(N * O):
-        w, c = ORDER[k // 2]
-        h = k % 2
-        s = who[w]
-        if w in ("own", "diag"):
-            for p, (w2, c2, h2, nh, nt) in enumerate(PARTS):
-                if (w2, c2) == (w, c) and h2 <= h < h2 + nh:
-                    once(te, "t", "pq%d" % p, 1)
+        w, o = ORDER[k]
+        s = by[w]
+        if part(w, o):
+            once(te, "t", "pq%d" % part(w, o)[0], 1)
         else:
-            once(te, "t", "r%d%d" % (s, c), (len(early) if c == 0 else 2) * nfar[w])
+            for kind in "qs":
+                once(te, "t", *comes[(kind, s, o)])
         if k >= 8:
             te.wait_ge(S["e%d" % (k - 8)], 1)
-        te.matmul_mx(T.ps[:, k % 8 * 512:k % 8 * 512 + TC], T["q%d%d" % (s, c)][:, h * CW:(h + 1) * CW],
-                     T["s%d%d" % (s, c)][:, h * CW:(h + 1) * CW], T.xq[:, :], T.xs[:, :], True, True).then_inc(S["m%d" % k], 1)
-    for k in range(0, N * O, 2):
-        sy.wait_ge(S["e%d" % k], 1)
-        sy.wait_ge(S["e%d" % (k + 1)], 1)
-        sy.dma_start(T.y[:, col(k):col(k) + 2 * TC], T.ys[:, col(k):col(k) + 2 * TC]).then_inc(S.st, 16)
-    sy.wait_ge(S.st, 16 * (N * O // 2))
+        te.matmul_mx(T.ps[:, k % 8 * 512:k % 8 * 512 + TC], T["q%d" % s][:, o * CW:(o + 1) * CW],
+                     T["s%d" % s][:, o * CW:(o + 1) * CW], T.xq[:, :], T.xs[:, :], True, True).then_inc(S["m%d" % k], 1)
+    nst = 0
+    for k in range(N * O):
+        w, o = ORDER[k]
+        ks = [ORDER.index((w, o - o % 2 + j)) for j in range(2)]
+        if max(ks) >= STORE or max(ks) - min(ks) > 2:
+            ks = [k]
+        if max(ks) == k:
+            for j in ks:
+                sy.wait_ge(S["e%d" % j], 1)
+            if nst == HOLD[0]:
+                sy.wait_ge(S.hold, 1)
+            c0 = col(ks[0])
+            sy.dma_start(T.y[:, c0:c0 + len(ks) * TC], T.ys[:, c0:c0 + len(ks) * TC]).then_inc(S.st, 16)
+            nst += 1
+    sy.wait_ge(S.st, 16 * nst)

from concourse.bass import DstId, RemoteDMATransfer
from concourse.mybir import dt, AluOpType, ActivationFunctionType

N, TC, O, K = 4, 256, 4, 256
CW = 128
NT = 4
LC = CW // 16

HOLD = (None, None)
PARTS = [("own", 0, 1, 1), ("own", 1, 1, 2), ("own", 2, 2, 2), ("plane", 2, 1, 4), ("plane", 3, 1, 4), ("diag", 3, 1, 4)]
LISTS = (1, 2, 2)
WAYS = {0: {"own": [("far", ["plane"]), ("near0", ["own.o0"]), ("near1", ["own.s0"])],
            "own.o0": [("far", ["diag"])], "own.s0": [("far", ["mate"])]},
        1: {"own": [("far", ["mate"])]},
        2: {"own": [("far", ["plane"]), ("near0", ["own.o0"]), ("near1", ["own.o1"])],
            "own.o0": [("far", ["diag"])], "own.o1": [("far", ["mate"])]}}
PIECES = [("q", "own", 0, 1, 2), ("q", "own", 1, 1, 0), ("s", "own", 0, 2, 0),
          ("q", "own", 2, 2, 1), ("s", "own", 2, 2, 1), ("q", "plane", 2, 1, 1), ("s", "plane", 2, 1, 1)]
GPSIMD = [("own", _i) for _i in range(len(PIECES))]
ORDER = [("own", 0), ("own", 1), ("own", 2), ("own", 3), ("plane", 0), ("plane", 1), ("plane", 2), ("plane", 3),
         ("mate", 2), ("mate", 3), ("mate", 0), ("mate", 1), ("diag", 0), ("diag", 1), ("diag", 2), ("diag", 3)]
SCALAR = [(0, 0), (0, 2), (0, 3), (1, 0), (1, 1), (2, 0), (2, 1), 0, 1, (3, 0), (4, 0), 2, (5, 0),
          3, 4, 5, 6, 7, 8, 9, 11, 13, 15]
VECTOR = [(0, 1), "p0", "p1", "x", "p2", "p3", "p4", "p5", 10, 12, 14]
STORE = 16

SCRATCH = {
    "cwb": ("sbuf", [128, O, 2, LC], "int32"),
    "bk0": ("sbuf", [128, NT * K], "bfloat16"),
    "bk1": ("sbuf", [128, NT * K], "bfloat16"),
    "xb": ("sbuf", [128, NT * TC], "bfloat16"),
    "xq": ("sbuf", [128, TC], "float8_e4m3fn_x4"),
    "xs": ("sbuf", [128, TC], "uint8"),
    "ys": ("sbuf", [128, N * O * TC], "float32"),
    "ps": ("psum", [128, 8 * 512], "float32"),
    "of1": ("sbuf", [128, O, 2, NT * LC], "uint16"),
    "li": ("sbuf", [128, O // 2, 2, 2 * LC], "uint16"),
    "of2": ("sbuf", [128, O // 2, 2, NT * 2 * LC], "uint16"),
}
SEMAPHORES = ["ldc", "ld0", "ld1", "ldx", "lst", "lst1", "lst2", "lstr", "sx", "sent", "st", "hold"]
for _s in range(N):
    SCRATCH["q%d" % _s] = ("sbuf", [128, O * CW], "float8_e4m3fn_x4")
    SCRATCH["s%d" % _s] = ("sbuf", [128, O * CW], "uint8")
    SEMAPHORES += ["r%s%d%d" % (_k, _s, _o) for _o in range(O) for _k in "qs"]
for _p in range(len(PARTS)):
    SCRATCH["a%d" % _p] = ("sbuf", [128, NT * CW * PARTS[_p][2]], "bfloat16")
    SCRATCH["w%d" % _p] = ("sbuf", [128, NT * CW * PARTS[_p][2]], "bfloat16")
    SEMAPHORES += ["pa%d%d" % (_p, _t) for _t in range(NT)] + ["pv%d" % _p, "pq%d" % _p]
FOREIGN = sorted(set(_p[0] for _p in PARTS) - {"own"})
for _w in FOREIGN:
    SCRATCH["of" + _w] = ("sbuf", [128, LISTS[2], 2, NT * LC] if LISTS[0] == 1 else [128, LISTS[2] // 2, 2, NT * 2 * LC],
                          "uint16")
    SEMAPHORES += ["l" + _w]
for _k in range(N * O):
    SEMAPHORES += ["m%d" % _k, "e%d" % _k]
RELS = ["own", "mate", "plane", "diag"]


def relation(topo, a, b):
    ca, cb = topo.chip(a), topo.chip(b)
    return "own" if a == b else "mate" if topo.mates(ca, cb) else "plane" if topo.same_plane(ca, cb) else "diag"


def rank_program(g, core, T, topo):
    S = T.sem
    who = [{relation(topo, T.cores[r], T.cores[s]): s for s in range(N)} for r in range(N)]
    named = []
    for r in range(N):
        names = {}
        for w in RELS:
            home = names[w] = T.cores[who[r][w]]
            mate = T.cores[who[who[r][w]]["mate"]]
            for key, same in (("o", False), ("s", True)):
                cs = [c for c in topo.cores_of(home) if c != home and (topo.die(c) == topo.die(home)) == same]
                cs.sort(key=lambda c: not topo.may_write(c, mate))
                for i, c in enumerate(cs):
                    names["%s.%s%d" % (w, key, i)] = c
        named.append(names)
    far = topo.engines(named[0]["own"], named[0]["mate"])
    near = [e for e in topo.engines(named[0]["own"], named[0]["own.o0"]) if e not in far]
    sets = {"far": far, "near": near, "all": far + near}
    for key in ("far", "near"):
        h = len(sets[key]) // 2
        sets[key + "0"], sets[key + "1"] = sets[key][:h], sets[key][h:]

    def transfer(src, dst, cores, sem, es):
        ids = [DstId(rid=topo.addr(c)[0], pnc=topo.addr(c)[1]) for c in cores]
        return RemoteDMATransfer(dst_ids=ids, dma_engine_mask=sum(1 << e for e in es), remote_sem=S[sem], srcs=[src],
                                 dsts=[dst] * len(ids))

    comes = {}
    for r in range(N):
        for kind, w, o, n, way in PIECES:
            for snd in WAYS[way]:
                for es, to in WAYS[way][snd]:
                    if core in [named[r][d] for d in to]:
                        for j in range(o, o + n):
                            comes[(kind, who[r][w], j)] = ("r%s%d%d" % (kind, who[r][w], o), len(sets[es]))
    nsent = [0]

    def part(w, o):
        return [p for p, (w2, o2, n, nt) in enumerate(PARTS) if w2 == w and o2 <= o < o2 + n]

    seen = {}

    def once(q, key, sem, n):
        if (key, sem) not in seen:
            seen[(key, sem)] = 1
            q.wait_ge(S[sem], n)

    def send(r, i, snd):
        kind, w, o, n, way = PIECES[i]
        s = who[r][w]
        src = T["%s%d" % (kind, s)][:, o * CW:(o + n) * CW]
        if kind == "q":
            src = src.bitcast(dt.uint8)
        for j in range(o, o + n):
            if snd != "own":
                once(g, "g", *comes[(kind, s, j)])
            else:
                once(g, "g", "pq%d" % part(w, j)[0], 1)
        g.remote_dma_fused([transfer(src, src, [named[r][d] for d in to], "r%s%d%d" % (kind, s, o), sets[es])
                            for es, to in WAYS[way][snd]], local_sem=S.sent)
        nsent[0] += sum(len(sets[es]) for es, to in WAYS[way][snd])

    me = T.rank_of(core)
    if me is None:
        for i in range(len(PIECES)):
            for snd in WAYS[PIECES[i][4]]:
                for r in range(N):
                    if named[r][snd] == core:
                        send(r, i, snd)
        if nsent[0]:
            g.wait_ge(S.sent, nsent[0])
        return
    v, a, te, sy = g.vector, g.scalar, g.tensor, g.sync
    by = who[me]
    nl = len(far) // max(1, len(FOREIGN))

    sy.dma_start(T.cwb[:], T.cw[:, :]).then_inc(S.ldc, 16)
    sy.dma_start(T.bk0[:, :], T.book[:, 0:NT * K]).then_inc(S.ld0, 16)
    sy.dma_start(T.bk1[:, :], T.book[:, NT * K:2 * NT * K]).then_inc(S.ld1, 16)
    sy.dma_start(T.xb[:, :], T.x[:, :]).then_inc(S.ldx, 16)

    if LISTS:
        lw, lo, ln = LISTS
        g.wait_ge(S.lst1 if lw == 1 else S.lst2, NT)
        src = T.of1[:, lo:lo + ln, :, :] if lw == 1 else T.of2[:, lo // 2:(lo + ln) // 2, :, :]
        g.remote_dma_fused([transfer(src, T["of" + w][:], [named[me][w]], "l" + w,
                                     far[i * nl:(i + 1) * nl]) for i, w in enumerate(FOREIGN)], local_sem=S.sent)
        nsent[0] += len(far)
    for snd, p in GPSIMD:
        send(by[snd], p, snd)
        if p == HOLD[1]:
            g.sem_inc(S.hold, 1)
    g.wait_ge(S.sent, nsent[0])

    def col(k):
        w, o = ORDER[k]
        return (by[w] * O + o) * TC

    def take(k):
        return T.ys[:, col(k):col(k) + TC], T.ps[:, k % 8 * 512:k % 8 * 512 + TC]

    def offsets(q, key, p, m, t, nt):
        w, o, n, _ = PARTS[p]
        if w == "own" and n == 1 and (nt > 1 or LISTS[0] == 1):
            once(q, key, "lst1", NT)
            return T.of1[:, o, m, t * LC:(t + nt) * LC]
        if w != "own" and LISTS[0] == 1:
            once(q, key, "l" + w, nl)
            return T["of" + w][:, o - LISTS[1], m, t * LC:(t + nt) * LC]
        if w == "own":
            once(q, key, "lst2", NT)
            of = T.of2
        else:
            once(q, key, "l" + w, nl)
            of, o = T["of" + w], o - LISTS[1]
        c0 = (2 * t + o % 2) * LC
        return of[:, o // 2, m, c0:c0 + n * nt * LC]

    def gather0(q, key, p, i):
        w, o, n, nt = PARTS[p]
        once(q, key, "ld0", 16)
        off = offsets(q, key, p, 0, i * nt, nt)
        return T["a%d" % p][:, i * nt * n * CW:(i + 1) * nt * n * CW], T.bk0[:, :].indirect(off)

    for it in SCALAR:
        if isinstance(it, int):
            a.wait_ge(S["m%d" % it], 1)
            dst, src = take(it)
            a.activation(dst, src, ActivationFunctionType.Copy).then_inc(S["e%d" % it], 1)
        else:
            dst, src = gather0(a, "a", *it)
            a.activation(dst, src, ActivationFunctionType.Copy).then_inc(S["pa%d%d" % it], 1)

    v.wait_ge(S.ldc, 16)

    def tables1():
        for t in range(NT):
            v.tensor_scalar(T.of1[:, :, :, t * LC:(t + 1) * LC], T.cwb[:, :, :, :], NT, t, AluOpType.mult,
                            AluOpType.add).then_inc(S.lst1, 1)

    def tables2():
        for m in range(2):
            v.tensor_scalar(T.li[:, :, m, :], T.cwb[:, :, m, :], NT, None, AluOpType.mult).then_inc(S.lst, 1)
        v.wait_ge(S.lst, 2)
        for t in range(NT):
            v.tensor_scalar(T.of2[:, :, :, 2 * t * LC:2 * (t + 1) * LC], T.li[:, :, :, :], t, None, AluOpType.add).then_inc(S.lst2, 1)

    if LISTS[0] == 1:
        tables1()
        if [p for p in PARTS if p[2] == 2]:
            tables2()
    else:
        tables2()
        if [p for p in PARTS if p[2] == 1 and p[3] > 1]:
            tables1()
    for it in VECTOR:
        if it == "x":
            v.wait_ge(S.ldx, 16)
            v.quantize_mx(T.xq[:, :], T.xs[:, :], T.xb[:, :]).then_inc(S.sx, 1)
        elif isinstance(it, int):
            v.wait_ge(S["m%d" % it], 1)
            dst, src = take(it)
            v.tensor_copy(dst, src).then_inc(S["e%d" % it], 1)
        elif isinstance(it, tuple):
            dst, src = gather0(v, "v", *it)
            v.tensor_copy(dst, src).then_inc(S["pa%d%d" % it], 1)
        else:
            p = int(it[1])
            w, o, n, nt = PARTS[p]
            A, W = T["a%d" % p], T["w%d" % p]
            once(v, "v", "ld1", 16)
            for t in {"p": range(NT), "q": [], "g": [int(it[-1])]}[it[0]]:
                off = offsets(v, "v", p, 1, t, 1)
                once(v, "v", "pa%d%d" % (p, t // nt), 1)
                v.tensor_tensor(W[:, t::NT], T.bk1[:, :].indirect(off), A[:, t * n * CW:(t + 1) * n * CW],
                                AluOpType.add).then_inc(S["pv%d" % p], 1)
            if it[0] == "g":
                continue
            v.wait_ge(S["pv%d" % p], NT)
            s = by[w]
            v.quantize_mx(T["q%d" % s][:, o * CW:(o + n) * CW], T["s%d" % s][:, o * CW:(o + n) * CW],
                          W[:, :]).then_inc(S["pq%d" % p], 1)

    te.wait_ge(S.sx, 1)
    for k in range(N * O):
        w, o = ORDER[k]
        s = by[w]
        if part(w, o):
            once(te, "t", "pq%d" % part(w, o)[0], 1)
        else:
            for kind in "qs":
                once(te, "t", *comes[(kind, s, o)])
        if k >= 8:
            te.wait_ge(S["e%d" % (k - 8)], 1)
        te.matmul_mx(T.ps[:, k % 8 * 512:k % 8 * 512 + TC], T["q%d" % s][:, o * CW:(o + 1) * CW],
                     T["s%d" % s][:, o * CW:(o + 1) * CW], T.xq[:, :], T.xs[:, :], True, True).then_inc(S["m%d" % k], 1)
    nst = 0
    for k in range(N * O):
        w, o = ORDER[k]
        ks = [ORDER.index((w, o - o % 2 + j)) for j in range(2)]
        if max(ks) >= STORE or max(ks) - min(ks) > 2:
            ks = [k]
        if max(ks) == k:
            for j in ks:
                sy.wait_ge(S["e%d" % j], 1)
            if nst == HOLD[0]:
                sy.wait_ge(S.hold, 1)
            c0 = col(ks[0])
            sy.dma_start(T.y[:, c0:c0 + len(ks) * TC], T.ys[:, c0:c0 + len(ks) * TC]).then_inc(S.st, 16)
            nst += 1
    sy.wait_ge(S.st, 16 * nst)
